import numpy as np
import ml_dtypes


def mxq(x, axis, fmt="e4m3"):
    dtype, down = {"e4m3": (ml_dtypes.float8_e4m3fn, 7), "e5m2": (ml_dtypes.float8_e5m2, 14)}[fmt]
    v = np.moveaxis(np.asarray(x, np.float32).astype(ml_dtypes.bfloat16).astype(np.float64), axis, -1)
    blocks = v.reshape(v.shape[:-1] + (-1, 32))
    amax = np.abs(blocks).max(-1, keepdims=True)
    byte = np.maximum(np.where(amax > 0, np.frexp(amax)[1] - 1 + 127, 0) - down, 1)
    scale = np.exp2(byte - 127.0)
    codes = (blocks / scale).astype(np.float32).astype(dtype).astype(np.float64)
    return np.moveaxis((codes * scale).reshape(v.shape), -1, axis)


WIDE = False


def mx_kscale(k):
    if not WIDE:
        return np.ones(k)
    levels = np.array([10, -10, 5, -5, 0])
    if k % 512:
        return np.exp2(np.random.permutation(np.resize(levels, k // 32))).repeat(32)
    a = np.empty((k // 512, 16))
    for p in range(k // 512):
        a[p, :8] = np.random.permutation(np.resize(levels, 8))
        for g in range(8):
            far = levels[np.abs(levels - a[p, g]) >= 10]
            a[p, g + 8] = far[np.random.randint(len(far))]
    return np.exp2(a.ravel()).repeat(32)


def f64(x):
    return np.asarray(x).astype(np.float64)


def striped(idx):
    return np.tile(idx.reshape(-1, 16).T, (8, 1)).astype(np.uint16)


def unstriped(offs):
    return offs[:16].T.reshape(-1).astype(np.int64)


def striped8(idx):
    return np.concatenate([x.reshape(-1, 16).T for x in idx]).astype(np.uint16)


def runs(offs, k):
    lists = np.stack([offs[16 * r : 16 * r + 16].T.reshape(-1) for r in range(8)]).astype(np.int64)
    return lists[np.arange(k) % 512 // 64]


def pack_weight(w):
    k, n = w.shape
    w = f64(np.asarray(w, np.float32).astype(ml_dtypes.bfloat16)).reshape(k // 32, 32, n)
    amax = np.abs(w).max(1)
    byte = np.clip(np.where(amax > 0, np.frexp(amax)[1] - 1 + 127 - 7, 1), 1, 254)
    scaled = (w * np.exp2(127.0 - byte)[:, None, :]).reshape(k, n).astype(np.float32)
    words = np.ascontiguousarray(scaled.reshape(k // 512, 128, 4, n).transpose(0, 1, 3, 2)).astype(ml_dtypes.float8_e4m3fn).view(np.uint8)
    return words, np.ascontiguousarray(byte.astype(np.uint8).reshape(k // 512, 16, n))


def unpack_weight(words, scales):
    g, p, n, _ = words.shape
    vals = np.ascontiguousarray(words).view(ml_dtypes.float8_e4m3fn).astype(np.float64) * np.repeat(np.exp2(scales.astype(np.float64) - 127.0), 8, axis=1)[..., None]
    return vals.transpose(0, 1, 3, 2).reshape(g * 512, n)


def sigmoid(v):
    return 1.0 / (1.0 + np.exp(-np.maximum(v, -700.0)))

def planes(y):
    n, m = y.shape
    v = y.astype(np.float32).astype(ml_dtypes.bfloat16).astype(np.float64).reshape(n // 32, 32, m)
    top = np.abs(v).max(1)
    byte = np.clip(np.where(top > 0, np.frexp(top)[1] - 1 + 127 - 7, 1), 1, 254)
    codes = (v * np.exp2(127.0 - byte)[:, None, :]).reshape(n, m).astype(np.float32).astype(ml_dtypes.float8_e4m3fn).view(np.uint8)
    words = codes.reshape(n // 512, 128, 4, m).transpose(0, 1, 3, 2)
    return np.ascontiguousarray(words), np.ascontiguousarray(byte.astype(np.uint8).reshape(n // 512, 16, m))


K, T, S, V, G, H, J = 512, 1024, 512, 512, 2048, 512, 512


def setup_inputs():
    n = np.random.standard_normal
    s = mx_kscale(K)[:, None]
    u = mx_kscale(S)
    packed_xT = pack_weight(n((K, T)) * s)
    packed_dT = pack_weight(n((K, G)) / s)
    packed_w1 = pack_weight(n((K, H)) / np.sqrt(K) / s)
    return {
        "x_words": packed_xT[0],
        "x_scales": packed_xT[1],
        "d_words": packed_dT[0],
        "d_scales": packed_dT[1],
        "w1_words": packed_w1[0],
        "w1_scales": packed_w1[1],
        "tab": n((H, J)).astype(np.float32),
        "ga": (np.random.uniform(0.5, 1.5, (H, 1)) * u[:, None]).astype(np.float32),
        "gb": (np.random.uniform(0.5, 1.5, (H, 1)) / u[:, None]).astype(np.float32),
        "offs": striped(np.random.permutation(T)[:S]),
        "k1": striped8(np.random.randint(0, G, (8, H))),
        "two": striped(np.random.permutation(T)[:V]),
        "n1": striped8(np.random.randint(0, J, (8, S))),
        "n2": striped8(np.stack([np.random.permutation(S) for _ in range(8)])),
        "n3": striped8(np.stack([np.random.permutation(V) for _ in range(8)])),
        "n4": striped8(np.stack([np.random.permutation(V) for _ in range(8)])),
        "n5": striped8(np.stack([np.random.permutation(V) for _ in range(8)])),
        "n6": striped8(np.stack([np.random.permutation(V) for _ in range(8)])),
    }


def reference(x_words, x_scales, d_words, d_scales, w1_words, w1_scales, tab, ga, gb, offs, k1, two, n1, n2, n3, n4, n5, n6):
    d_k1 = unpack_weight(d_words, d_scales)[np.arange(K)[:, None], runs(k1, K)]
    xq = unpack_weight(x_words, x_scales)[:, unstriped(offs)]
    a = 0.0625 * (d_k1.T @ xq)
    z = f64(ga) * (np.maximum(a + f64(tab)[np.arange(H)[:, None], runs(n1, H)], a[np.arange(H)[:, None], runs(n2, H)]))
    x_two = unpack_weight(x_words, x_scales)[:, unstriped(two)]
    b = unpack_weight(w1_words, w1_scales).T @ x_two
    z2 = f64(gb) * (b - (b[np.arange(H)[:, None], runs(n3, H)]))
    s = 0.0625 * ((mxq(z, 0, "e4m3").T @ mxq(z2, 0, "e4m3")))
    pa = s[np.arange(S)[:, None], runs(n4, S)]
    out_0 = pa + (sigmoid(s[np.arange(S)[:, None], runs(n5, S)])) * (s[np.arange(S)[:, None], runs(n6, S)] - pa)
    return (out_0,) + planes(out_0)

@@ -1,0 +1,235 @@
+from contextlib import ExitStack
+
+import concourse.mybir as mybir
+
+F32 = mybir.dt.float32
+BF16 = mybir.dt.bfloat16
+I32 = mybir.dt.int32
+U32 = mybir.dt.uint32
+U16 = mybir.dt.uint16
+U8 = mybir.dt.uint8
+FP8X4 = mybir.dt.float8_e4m3fn_x4
+ALU = mybir.AluOpType
+ACT = mybir.ActivationFunctionType
+
+P = 128
+PACK = 4
+N = 512
+T = 1024
+G = 2048
+HALF = 256
+SIXTEENTH = 0.0625
+OUT_CHUNKS = ((0, 256), (256, 128), (384, 128))
+
+FLOPS = 3 * 2 * 512 * 512 * 512
+
+
+def tile_picked_ckqkinddiflerp_none_po_kernel(
+    tc, x_words, x_scales, d_words, d_scales, w1_words, w1_scales, tab, ga, gb,
+    offs, k1, two, n1, n2, n3, n4, n5, n6, out_0, out_1, out_2,
+):
+    nc = tc.nc
+    with ExitStack() as ctx:
+        keep = ctx.enter_context(tc.tile_pool(name="keep", bufs=1))
+        psum = ctx.enter_context(tc.psum_pool(name="psum", bufs=1))
+
+        def sb(name, shape, dtype):
+            return keep.tile(shape, dtype, name=name, align_bytes=64)
+
+        def load_list(name, src):
+            lst = keep.tile([P, N // 16], U16, name=name)
+            nc.sync.dma_start(lst[:], src)
+            return lst
+
+        def words_of(src):
+            return src[0].rearrange("p n r -> p (n r)").bitcast(I32)
+
+        def entries(lst, start, count):
+            return lst[:, start // 16 : (start + count) // 16]
+
+        x_w = sb("x_w", [P, T], U32)
+        d_w = sb("d_w", [P, G], U32)
+        w1_w = sb("w1_w", [P, N], U32)
+        x_s = sb("x_s", [P, T], U8)
+        d_s = sb("d_s", [P, G], U8)
+        w1_s = sb("w1_s", [P, N], U8)
+        tab_t = [sb("tab_%d" % t, [P, N], F32) for t in range(PACK)]
+        ga_t = sb("ga_t", [P, PACK], F32)
+        gb_t = sb("gb_t", [P, PACK], F32)
+        tab_rows = tab.rearrange("(p t) c -> p t c", t=PACK)
+
+        nc.gpsimd.memset(x_s[:].bitcast(I32), 0)
+        nc.gpsimd.memset(w1_s[:].bitcast(I32), 0)
+        nc.vector.memset(d_s[:].bitcast(I32), 0)
+
+        def load_scale_rows(queue, plane, src):
+            for q in range(4):
+                queue.dma_start(plane[32 * q : 32 * q + 4, :].bitcast(I32), src[0, 4 * q : 4 * q + 4, :].bitcast(I32))
+
+        load_scale_rows(nc.scalar, x_s, x_scales)
+        two_l = load_list("two_l", two)
+        nc.sync.dma_start(x_w[:].bitcast(I32), words_of(x_words))
+        n1_l = load_list("n1_l", n1)
+        nc.sync.dma_start(tab_t[0][:], tab_rows[:, 0, :])
+        nc.sync.dma_start(w1_w[:].bitcast(I32), words_of(w1_words))
+        load_scale_rows(nc.sync, w1_s, w1_scales)
+        nc.gpsimd.dma_start(ga_t[:], ga.rearrange("(p t) o -> p (t o)", t=PACK))
+        nc.gpsimd.dma_start(gb_t[:], gb.rearrange("(p t) o -> p (t o)", t=PACK))
+        k1_l = load_list("k1_l", k1)
+        d_rows = d_scales[0].rearrange("(r e) n -> e r n", e=2)
+        for e in range(2):
+            nc.sync.dma_start(d_s[e:P:16, :].bitcast(I32), d_rows[e].bitcast(I32))
+        nc.sync.dma_start(tab_t[1][:], tab_rows[:, 1, :])
+        n3_l = load_list("n3_l", n3)
+        offs_l = load_list("offs_l", offs)
+        nc.sync.dma_start(d_w[:].bitcast(I32), words_of(d_words))
+        nc.sync.dma_start(tab_t[2][:], tab_rows[:, 2, :])
+        nc.sync.dma_start(tab_t[3][:], tab_rows[:, 3, :])
+        n2_l = load_list("n2_l", n2)
+        n4_l = load_list("n4_l", n4)
+        n6_l = load_list("n6_l", n6)
+        n5_l = load_list("n5_l", n5)
+
+        sign_a = sb("sign_a", [P, PACK], F32)
+        abs_ga = sb("abs_ga", [P, PACK], F32)
+        a_gain = sb("a_gain", [P, PACK], F32)
+        b_gain = sb("b_gain", [P, PACK], F32)
+        twice = sb("twice", [P, PACK], F32)
+        nc.gpsimd.tensor_scalar(twice[:], ga_t[:], 0.0, 2.0, ALU.is_ge, ALU.mult)
+        nc.gpsimd.tensor_scalar(sign_a[:], twice[:], 1.0, -1.0, ALU.mult, ALU.add)
+        nc.gpsimd.tensor_tensor(b_gain[:], gb_t[:], sign_a[:], ALU.mult)
+        nc.gpsimd.tensor_tensor(abs_ga[:], ga_t[:], sign_a[:], ALU.mult)
+        nc.gpsimd.tensor_scalar(a_gain[:], abs_ga[:], SIXTEENTH, 0.0, ALU.mult, ALU.add)
+
+        def deal(dst, src):
+            nc.vector.tensor_copy(
+                dst[:].rearrange("p (t m) -> p t m", t=PACK), src[:].rearrange("p (m t) -> p t m", t=PACK)
+            )
+
+        def pick(name, table, lst, dtype):
+            got = sb(name, [P, N], dtype)
+            nc.vector.tensor_copy(got[:], table[:].indirect(lst[:]))
+            return got
+
+        def product(bank, t, lhs_w, lhs_s, rhs_w, rhs_s):
+            acc = psum.tile([P, N], F32, name="bank%d" % bank)
+            cols = slice(P * t, P * (t + 1))
+            nc.tensor.matmul_mx(
+                out=acc[:], lhsT=lhs_w[:, cols].bitcast(FP8X4), lhsT_scale=lhs_s[:, cols],
+                rhs=rhs_w[:].bitcast(FP8X4), rhs_scale=rhs_s[:], start=True, stop=True,
+            )
+            return acc
+
+        def fetch(dst, window, lst, start, count, func):
+            nc.scalar.activation(dst, window[:].indirect(entries(lst, start, count)), func)
+
+        xt_s = pick("xt_s", x_s, two_l, U8)
+        xt_w = pick("xt_w", x_w, two_l, U32)
+        w1_wd = sb("w1_wd", [P, N], U32)
+        w1_sd = sb("w1_sd", [P, N], U8)
+        deal(w1_wd, w1_w)
+        deal(w1_sd, w1_s)
+
+        dk_s = pick("dk_s", d_s, k1_l, U8)
+        dk_sd = sb("dk_sd", [P, N], U8)
+        deal(dk_sd, dk_s)
+        for e in range(2):
+            nc.gpsimd.dma_start(dk_sd[2 + e : P : 32, :].bitcast(I32), dk_sd[16 + e : P : 32, :].bitcast(I32))
+
+        tab_g = sb("tab_g", [P, PACK, N], F32)
+        for t in range(2):
+            for h in range(0, N, HALF):
+                fetch(tab_g[:, t, h : h + HALF], tab_t[t], n1_l, h, HALF, ACT.Copy)
+
+        b_t = [sb("b_%d" % t, [P, N], F32) for t in range(PACK)]
+        b_all = sb("b_all", [P, PACK, N], F32)
+        b_g = sb("b_g", [P, PACK, N], F32)
+        b_acc = [product(t, t, w1_wd, w1_sd, xt_w, xt_s) for t in range(PACK)]
+
+        xo_w = pick("xo_w", x_w, offs_l, U32)
+        xo_s = pick("xo_s", x_s, offs_l, U8)
+        dk_w = pick("dk_w", d_w, k1_l, U32)
+        dk_wd = sb("dk_wd", [P, N], U32)
+        deal(dk_wd, dk_w)
+        a_acc = [product(PACK + t, t, dk_wd, dk_sd, xo_w, xo_s) for t in range(PACK)]
+
+        for t in range(PACK):
+            nc.scalar.activation(b_t[t][:], b_acc[t][:], ACT.Copy, scale=b_gain[:, t : t + 1])
+            for h in range(0, N, HALF):
+                fetch(b_g[:, t, h : h + HALF], b_t[t], n3_l, h, HALF, ACT.Copy)
+        for t in range(2, PACK):
+            for h in range(0, N, HALF):
+                fetch(tab_g[:, t, h : h + HALF], tab_t[t], n1_l, h, HALF, ACT.Copy)
+
+        a_t = [sb("a_%d" % t, [P, N], F32) for t in range(PACK)]
+        a_g = sb("a_g", [P, PACK, N], F32)
+        a_sum = sb("a_sum", [P, PACK, N], F32)
+        for t in range(PACK):
+            nc.scalar.activation(a_t[t][:], a_acc[t][:], ACT.Copy, scale=a_gain[:, t : t + 1])
+        for t in range(PACK):
+            nc.vector.scalar_tensor_tensor(
+                b_all[:, t, :], b_acc[t][:], b_gain[:, t : t + 1], b_g[:, t, :], ALU.mult, ALU.subtract
+            )
+        z2_h = sb("z2_h", [P, N, PACK], BF16)
+        nc.vector.tensor_copy(
+            z2_h[:].rearrange("p (c i) t -> p c t i", i=4), b_all[:].rearrange("p t (c i) -> p c t i", i=4)
+        )
+        for h in range(0, N, HALF):
+            for t in range(PACK):
+                fetch(a_g[:, t, h : h + HALF], a_t[t], n2_l, h, HALF, ACT.Copy)
+        for t in range(PACK):
+            nc.vector.scalar_tensor_tensor(
+                a_sum[:, t, :], tab_g[:, t, :], abs_ga[:, t : t + 1], a_t[t][:], ALU.mult, ALU.add
+            )
+        z2_w = sb("z2_w", [P, N], U32)
+        z2_s = sb("z2_s", [P, N], U8)
+        nc.vector.quantize_mx(out=z2_w[:].bitcast(FP8X4), scales=z2_s[:], in_=z2_h[:].rearrange("p c t -> p (c t)"))
+
+        z_h = sb("z_h", [P, PACK, P, PACK], BF16)
+        for h in range(0, N, HALF):
+            m = slice(h // PACK, (h + HALF) // PACK)
+            nc.vector.tensor_tensor(
+                z_h[:, :, m, :].rearrange("p u m t -> p m t u"),
+                a_sum[:, :, h : h + HALF].rearrange("p t (m u) -> p m t u", u=PACK),
+                a_g[:, :, h : h + HALF].rearrange("p t (m u) -> p m t u", u=PACK),
+                ALU.max,
+            )
+        z_w = sb("z_w", [P, N], U32)
+        z_s = sb("z_s", [P, N], U8)
+        nc.vector.quantize_mx(out=z_w[:].bitcast(FP8X4), scales=z_s[:], in_=z_h[:].rearrange("p u m t -> p (u m t)"))
+
+        s_t = [sb("s_%d" % t, [P, N], F32) for t in range(PACK)]
+        for t in range(PACK):
+            acc = product(t, t, z_w, z_s, z2_w, z2_s)
+            nc.vector.tensor_scalar(s_t[t][:], acc[:], SIXTEENTH, None, ALU.mult)
+
+        y_rows = out_0.rearrange("(p t) c -> p t c", t=PACK)
+        y_w = sb("y_w", [P, N], U32)
+        y_s = sb("y_s", [P, N], U8)
+        for c0, width in OUT_CHUNKS:
+            near = sb("near_%d" % c0, [P, PACK, width], F32)
+            far = sb("far_%d" % c0, [P, PACK, width], F32)
+            gate = sb("gate_%d" % c0, [P, PACK, width], F32)
+            diff = sb("diff_%d" % c0, [P, PACK, width], F32)
+            step = sb("step_%d" % c0, [P, PACK, width], F32)
+            y = sb("y_%d" % c0, [P, PACK, width], F32)
+            y_h = sb("y_h_%d" % c0, [P, width, PACK], BF16)
+            for t in range(PACK):
+                fetch(near[:, t, :], s_t[t], n4_l, c0, width, ACT.Copy)
+                fetch(far[:, t, :], s_t[t], n6_l, c0, width, ACT.Copy)
+                fetch(gate[:, t, :], s_t[t], n5_l, c0, width, ACT.Sigmoid)
+                nc.vector.tensor_tensor(diff[:, t, :], far[:, t, :], near[:, t, :], ALU.subtract)
+                nc.vector.tensor_tensor(step[:, t, :], diff[:, t, :], gate[:, t, :], ALU.mult)
+                nc.vector.tensor_tensor(y[:, t, :], step[:, t, :], near[:, t, :], ALU.add)
+            cols = slice(c0, c0 + width)
+            nc.sync.dma_start(y_rows[:, :, cols], y[:])
+            nc.vector.tensor_copy(
+                y_h[:].rearrange("p (c i) t -> p c t i", i=4), y[:].rearrange("p t (c i) -> p c t i", i=4)
+            )
+            nc.vector.quantize_mx(
+                out=y_w[:, cols].bitcast(FP8X4), scales=y_s[:, cols], in_=y_h[:].rearrange("p c t -> p (c t)")
+            )
+            nc.sync.dma_start(words_of(out_1)[:, cols], y_w[:, cols].bitcast(I32))
+        for q in range(4):
+            queue = nc.sync if q % 2 else nc.scalar
+            queue.dma_start(out_2[0, 4 * q : 4 * q + 4, :].bitcast(I32), y_s[32 * q : 32 * q + 4, :].bitcast(I32))

@@ -19,7 +19,9 @@ T = 1024
 G = 2048
 HALF = 256
 SIXTEENTH = 0.0625
-OUT_CHUNKS = ((0, 256), (256, 128), (384, 128))
+WIDE = 2 * N
+GATE_FIRST = (0, 1, 2)
+CHUNKS = ((0, 256), (256, 128), (384, 128))
 
 FLOPS = 3 * 2 * 512 * 512 * 512
 
@@ -33,8 +35,8 @@ def tile_picked_ckqkinddiflerp_none_po_kernel(
         keep = ctx.enter_context(tc.tile_pool(name="keep", bufs=1))
         psum = ctx.enter_context(tc.psum_pool(name="psum", bufs=1))
 
-        def sb(name, shape, dtype):
-            return keep.tile(shape, dtype, name=name, align_bytes=64)
+        def sb(name, shape, dtype, tag=None):
+            return keep.tile(shape, dtype, name=name, tag=tag or name, align_bytes=64)
 
         def load_list(name, src):
             lst = keep.tile([P, N // 16], U16, name=name)
@@ -53,13 +55,15 @@ def tile_picked_ckqkinddiflerp_none_po_kernel(
         x_s = sb("x_s", [P, T], U8)
         d_s = sb("d_s", [P, G], U8)
         w1_s = sb("w1_s", [P, N], U8)
-        tab_t = [sb("tab_%d" % t, [P, N], F32) for t in range(PACK)]
+        tab_t = [sb("tab_%d" % t, [P, WIDE], F32, tag="window_%d" % t) for t in range(PACK)]
         ga_t = sb("ga_t", [P, PACK], F32)
         gb_t = sb("gb_t", [P, PACK], F32)
         tab_rows = tab.rearrange("(p t) c -> p t c", t=PACK)
 
+        warm = sb("warm", [P, 1], F32)
         nc.gpsimd.memset(x_s[:].bitcast(I32), 0)
         nc.gpsimd.memset(w1_s[:].bitcast(I32), 0)
+        nc.vector.memset(warm[:], 0.0)
         nc.vector.memset(d_s[:].bitcast(I32), 0)
 
         def load_scale_rows(queue, plane, src):
@@ -67,47 +71,39 @@ def tile_picked_ckqkinddiflerp_none_po_kernel(
                 queue.dma_start(plane[32 * q : 32 * q + 4, :].bitcast(I32), src[0, 4 * q : 4 * q + 4, :].bitcast(I32))
 
         load_scale_rows(nc.scalar, x_s, x_scales)
+        nc.scalar.activation(warm[:], warm[:], ACT.Sigmoid)
+        nc.gpsimd.dma_start(ga_t[:], ga.rearrange("(p t) o -> p (t o)", t=PACK))
+        nc.gpsimd.dma_start(gb_t[:], gb.rearrange("(p t) o -> p (t o)", t=PACK))
         two_l = load_list("two_l", two)
         nc.sync.dma_start(x_w[:].bitcast(I32), words_of(x_words))
         n1_l = load_list("n1_l", n1)
-        nc.sync.dma_start(tab_t[0][:], tab_rows[:, 0, :])
+        nc.sync.dma_start(tab_t[0][:, :N], tab_rows[:, 0, :])
         nc.sync.dma_start(w1_w[:].bitcast(I32), words_of(w1_words))
+        nc.sync.dma_start(tab_t[1][:, :N], tab_rows[:, 1, :])
         load_scale_rows(nc.sync, w1_s, w1_scales)
-        nc.gpsimd.dma_start(ga_t[:], ga.rearrange("(p t) o -> p (t o)", t=PACK))
-        nc.gpsimd.dma_start(gb_t[:], gb.rearrange("(p t) o -> p (t o)", t=PACK))
         k1_l = load_list("k1_l", k1)
-        d_rows = d_scales[0].rearrange("(r e) n -> e r n", e=2)
-        for e in range(2):
-            nc.sync.dma_start(d_s[e:P:16, :].bitcast(I32), d_rows[e].bitcast(I32))
-        nc.sync.dma_start(tab_t[1][:], tab_rows[:, 1, :])
-        n3_l = load_list("n3_l", n3)
-        offs_l = load_list("offs_l", offs)
+        nc.sync.dma_start(d_s[0:P:8, :].bitcast(I32), d_scales[0].bitcast(I32))
         nc.sync.dma_start(d_w[:].bitcast(I32), words_of(d_words))
-        nc.sync.dma_start(tab_t[2][:], tab_rows[:, 2, :])
-        nc.sync.dma_start(tab_t[3][:], tab_rows[:, 3, :])
+        offs_l = load_list("offs_l", offs)
+        n3_l = load_list("n3_l", n3)
         n2_l = load_list("n2_l", n2)
+        nc.sync.dma_start(tab_t[2][:, :N], tab_rows[:, 2, :])
+        nc.sync.dma_start(tab_t[3][:, :N], tab_rows[:, 3, :])
         n4_l = load_list("n4_l", n4)
         n6_l = load_list("n6_l", n6)
         n5_l = load_list("n5_l", n5)
 
-        sign_a = sb("sign_a", [P, PACK], F32)
         abs_ga = sb("abs_ga", [P, PACK], F32)
         a_gain = sb("a_gain", [P, PACK], F32)
         b_gain = sb("b_gain", [P, PACK], F32)
-        twice = sb("twice", [P, PACK], F32)
-        nc.gpsimd.tensor_scalar(twice[:], ga_t[:], 0.0, 2.0, ALU.is_ge, ALU.mult)
-        nc.gpsimd.tensor_scalar(sign_a[:], twice[:], 1.0, -1.0, ALU.mult, ALU.add)
-        nc.gpsimd.tensor_tensor(b_gain[:], gb_t[:], sign_a[:], ALU.mult)
-        nc.gpsimd.tensor_tensor(abs_ga[:], ga_t[:], sign_a[:], ALU.mult)
-        nc.gpsimd.tensor_scalar(a_gain[:], abs_ga[:], SIXTEENTH, 0.0, ALU.mult, ALU.add)
 
         def deal(dst, src):
             nc.vector.tensor_copy(
                 dst[:].rearrange("p (t m) -> p t m", t=PACK), src[:].rearrange("p (m t) -> p t m", t=PACK)
             )
 
-        def pick(name, table, lst, dtype):
-            got = sb(name, [P, N], dtype)
+        def pick(name, table, lst, dtype, tag=None):
+            got = sb(name, [P, N], dtype, tag)
             nc.vector.tensor_copy(got[:], table[:].indirect(lst[:]))
             return got
 
@@ -130,54 +126,59 @@ def tile_picked_ckqkinddiflerp_none_po_kernel(
         deal(w1_wd, w1_w)
         deal(w1_sd, w1_s)
 
+        half_sign = sb("half_sign", [P, PACK], F32, tag="w1_s")
+        nc.vector.tensor_scalar(half_sign[:], ga_t[:], 0.0, 0.5, ALU.is_ge, ALU.subtract)
+        nc.vector.scalar_tensor_tensor(b_gain[:], half_sign[:], 2.0, gb_t[:], ALU.mult, ALU.mult)
+        nc.vector.scalar_tensor_tensor(abs_ga[:], half_sign[:], 2.0, ga_t[:], ALU.mult, ALU.mult)
+        nc.vector.scalar_tensor_tensor(a_gain[:], half_sign[:], 2.0 * SIXTEENTH, ga_t[:], ALU.mult, ALU.mult)
+
         dk_s = pick("dk_s", d_s, k1_l, U8)
         dk_sd = sb("dk_sd", [P, N], U8)
         deal(dk_sd, dk_s)
-        for e in range(2):
-            nc.gpsimd.dma_start(dk_sd[2 + e : P : 32, :].bitcast(I32), dk_sd[16 + e : P : 32, :].bitcast(I32))
+        for r in range(1, 4):
+            nc.sync.dma_start(dk_sd[r:P:32, :].bitcast(I32), dk_sd[8 * r : P : 32, :].bitcast(I32))
 
         tab_g = sb("tab_g", [P, PACK, N], F32)
         for t in range(2):
-            for h in range(0, N, HALF):
-                fetch(tab_g[:, t, h : h + HALF], tab_t[t], n1_l, h, HALF, ACT.Copy)
+            fetch(tab_g[:, t, :], tab_t[t], n1_l, 0, N, ACT.Copy)
 
-        b_t = [sb("b_%d" % t, [P, N], F32) for t in range(PACK)]
-        b_all = sb("b_all", [P, PACK, N], F32)
-        b_g = sb("b_g", [P, PACK, N], F32)
         b_acc = [product(t, t, w1_wd, w1_sd, xt_w, xt_s) for t in range(PACK)]
 
-        xo_w = pick("xo_w", x_w, offs_l, U32)
+        xo_w = pick("xo_w", x_w, offs_l, U32, tag="held")
         xo_s = pick("xo_s", x_s, offs_l, U8)
         dk_w = pick("dk_w", d_w, k1_l, U32)
         dk_wd = sb("dk_wd", [P, N], U32)
         deal(dk_wd, dk_w)
         a_acc = [product(PACK + t, t, dk_wd, dk_sd, xo_w, xo_s) for t in range(PACK)]
 
+        b_g = sb("b_g", [P, PACK, N], F32)
         for t in range(PACK):
-            nc.scalar.activation(b_t[t][:], b_acc[t][:], ACT.Copy, scale=b_gain[:, t : t + 1])
-            for h in range(0, N, HALF):
-                fetch(b_g[:, t, h : h + HALF], b_t[t], n3_l, h, HALF, ACT.Copy)
+            b_t = sb("b_%d" % t, [P, WIDE], F32, tag="window_%d" % (1 - t) if t < 2 else None)
+            nc.scalar.activation(b_t[:, :N], b_acc[t][:], ACT.Copy, scale=b_gain[:, t : t + 1])
+            fetch(b_g[:, t, :], b_t, n3_l, 0, N, ACT.Copy)
         for t in range(2, PACK):
-            for h in range(0, N, HALF):
-                fetch(tab_g[:, t, h : h + HALF], tab_t[t], n1_l, h, HALF, ACT.Copy)
+            fetch(tab_g[:, t, :], tab_t[t], n1_l, 0, N, ACT.Copy)
 
         a_t = [sb("a_%d" % t, [P, N], F32) for t in range(PACK)]
         a_g = sb("a_g", [P, PACK, N], F32)
         a_sum = sb("a_sum", [P, PACK, N], F32)
-        for t in range(PACK):
-            nc.scalar.activation(a_t[t][:], a_acc[t][:], ACT.Copy, scale=a_gain[:, t : t + 1])
+        for t in range(PACK - 1):
+            nc.vector.tensor_scalar(a_t[t][:], a_acc[t][:], a_gain[:, t : t + 1], None, ALU.mult)
+        nc.scalar.activation(a_t[3][:], a_acc[3][:], ACT.Copy, scale=a_gain[:, 3:4])
+        b_all = sb("b_all", [P, PACK, N], F32, tag="held")
         for t in range(PACK):
             nc.vector.scalar_tensor_tensor(
                 b_all[:, t, :], b_acc[t][:], b_gain[:, t : t + 1], b_g[:, t, :], ALU.mult, ALU.subtract
             )
+        for h, width in CHUNKS:
+            for t in range(PACK):
+                fetch(a_g[:, t, h : h + width], a_t[t], n2_l, h, width, ACT.Copy)
+        nc.vector.scalar_tensor_tensor(a_sum[:, 0, :], tab_g[:, 0, :], abs_ga[:, 0:1], a_t[0][:], ALU.mult, ALU.add)
         z2_h = sb("z2_h", [P, N, PACK], BF16)
         nc.vector.tensor_copy(
             z2_h[:].rearrange("p (c i) t -> p c t i", i=4), b_all[:].rearrange("p t (c i) -> p c t i", i=4)
         )
-        for h in range(0, N, HALF):
-            for t in range(PACK):
-                fetch(a_g[:, t, h : h + HALF], a_t[t], n2_l, h, HALF, ACT.Copy)
-        for t in range(PACK):
+        for t in range(1, PACK):
             nc.vector.scalar_tensor_tensor(
                 a_sum[:, t, :], tab_g[:, t, :], abs_ga[:, t : t + 1], a_t[t][:], ALU.mult, ALU.add
             )
@@ -186,50 +187,75 @@ def tile_picked_ckqkinddiflerp_none_po_kernel(
         nc.vector.quantize_mx(out=z2_w[:].bitcast(FP8X4), scales=z2_s[:], in_=z2_h[:].rearrange("p c t -> p (c t)"))
 
         z_h = sb("z_h", [P, PACK, P, PACK], BF16)
-        for h in range(0, N, HALF):
-            m = slice(h // PACK, (h + HALF) // PACK)
+        for h, width in CHUNKS:
+            m = slice(h // PACK, (h + width) // PACK)
             nc.vector.tensor_tensor(
                 z_h[:, :, m, :].rearrange("p u m t -> p m t u"),
-                a_sum[:, :, h : h + HALF].rearrange("p t (m u) -> p m t u", u=PACK),
-                a_g[:, :, h : h + HALF].rearrange("p t (m u) -> p m t u", u=PACK),
+                a_sum[:, :, h : h + width].rearrange("p t (m u) -> p m t u", u=PACK),
+                a_g[:, :, h : h + width].rearrange("p t (m u) -> p m t u", u=PACK),
                 ALU.max,
             )
         z_w = sb("z_w", [P, N], U32)
         z_s = sb("z_s", [P, N], U8)
-        nc.vector.quantize_mx(out=z_w[:].bitcast(FP8X4), scales=z_s[:], in_=z_h[:].rearrange("p u m t -> p (u m t)"))
+        for u in range(PACK):
+            cols = slice(P * u, P * (u + 1))
+            nc.vector.quantize_mx(
+                out=z_w[:, cols].bitcast(FP8X4), scales=z_s[:, cols], in_=z_h[:, u].rearrange("p m t -> p (m t)")
+            )
 
-        s_t = [sb("s_%d" % t, [P, N], F32) for t in range(PACK)]
-        for t in range(PACK):
-            acc = product(t, t, z_w, z_s, z2_w, z2_s)
-            nc.vector.tensor_scalar(s_t[t][:], acc[:], SIXTEENTH, None, ALU.mult)
+        s_t = [sb("s_%d" % t, [P, WIDE if t in GATE_FIRST else N], F32) for t in range(PACK)]
+        s_acc = [product(t, t, z_w, z_s, z2_w, z2_s) for t in range(PACK)]
+        nc.scalar.activation(s_t[0][:, :N], s_acc[0][:], ACT.Copy, scale=SIXTEENTH)
+        for t in range(1, PACK):
+            nc.vector.tensor_scalar(s_t[t][:, :N], s_acc[t][:], SIXTEENTH, None, ALU.mult)
 
         y_rows = out_0.rearrange("(p t) c -> p t c", t=PACK)
         y_w = sb("y_w", [P, N], U32)
         y_s = sb("y_s", [P, N], U8)
-        for c0, width in OUT_CHUNKS:
-            near = sb("near_%d" % c0, [P, PACK, width], F32)
-            far = sb("far_%d" % c0, [P, PACK, width], F32)
-            gate = sb("gate_%d" % c0, [P, PACK, width], F32)
-            diff = sb("diff_%d" % c0, [P, PACK, width], F32)
-            step = sb("step_%d" % c0, [P, PACK, width], F32)
-            y = sb("y_%d" % c0, [P, PACK, width], F32)
-            y_h = sb("y_h_%d" % c0, [P, width, PACK], BF16)
-            for t in range(PACK):
-                fetch(near[:, t, :], s_t[t], n4_l, c0, width, ACT.Copy)
-                fetch(far[:, t, :], s_t[t], n6_l, c0, width, ACT.Copy)
-                fetch(gate[:, t, :], s_t[t], n5_l, c0, width, ACT.Sigmoid)
-                nc.vector.tensor_tensor(diff[:, t, :], far[:, t, :], near[:, t, :], ALU.subtract)
-                nc.vector.tensor_tensor(step[:, t, :], diff[:, t, :], gate[:, t, :], ALU.mult)
-                nc.vector.tensor_tensor(y[:, t, :], step[:, t, :], near[:, t, :], ALU.add)
+        near = sb("near", [P, PACK, N], F32)
+        far = sb("far", [P, PACK, N], F32)
+        gate = sb("gate", [P, PACK, N], F32)
+        diff = sb("diff", [P, PACK, N], F32)
+        step = sb("step", [P, PACK, N], F32)
+        y = sb("y", [P, PACK, N], F32)
+        y_h = sb("y_h", [P, N, PACK], BF16)
+
+        def blend(t, c0, width):
             cols = slice(c0, c0 + width)
-            nc.sync.dma_start(y_rows[:, :, cols], y[:])
+            fetch(near[:, t, cols], s_t[t], n4_l, c0, width, ACT.Copy)
+            fetch(far[:, t, cols], s_t[t], n6_l, c0, width, ACT.Copy)
+            nc.vector.tensor_tensor(diff[:, t, cols], far[:, t, cols], near[:, t, cols], ALU.subtract)
+            if t in GATE_FIRST:
+                nc.vector.tensor_tensor(
+                    step[:, t, cols], gate_t[t][:].indirect(entries(n5_l, c0, width)), diff[:, t, cols], ALU.mult
+                )
+            else:
+                fetch(gate[:, t, cols], s_t[t], n5_l, c0, width, ACT.Sigmoid)
+                nc.vector.tensor_tensor(step[:, t, cols], diff[:, t, cols], gate[:, t, cols], ALU.mult)
+            nc.vector.tensor_tensor(y[:, t, cols], step[:, t, cols], near[:, t, cols], ALU.add)
+
+        last = PACK - 1
+        gate_t = [sb("gate_%d" % t, [P, WIDE], F32) for t in GATE_FIRST]
+        for t in range(last):
+            nc.scalar.activation(gate_t[t][:, :N], s_acc[t][:], ACT.Sigmoid, scale=SIXTEENTH)
+            for h, width in ((0, HALF), (HALF, HALF)) if t == 0 else ((0, N),):
+                blend(t, h, width)
+            nc.sync.dma_start(y_rows[:, t, :], y[:, t, :])
+        for c, (h, width) in enumerate(CHUNKS):
+            blend(last, h, width)
+            cols = slice(h, h + width)
+            if c != 1:
+                stored = slice(0, HALF) if c == 0 else slice(HALF, N)
+                nc.sync.dma_start(y_rows[:, last, stored], y[:, last, stored])
             nc.vector.tensor_copy(
-                y_h[:].rearrange("p (c i) t -> p c t i", i=4), y[:].rearrange("p t (c i) -> p c t i", i=4)
+                y_h[:, cols, :].rearrange("p (c i) t -> p c t i", i=4), y[:, :, cols].rearrange("p t (c i) -> p c t i", i=4)
             )
             nc.vector.quantize_mx(
-                out=y_w[:, cols].bitcast(FP8X4), scales=y_s[:, cols], in_=y_h[:].rearrange("p c t -> p (c t)")
+                out=y_w[:, cols].bitcast(FP8X4), scales=y_s[:, cols], in_=y_h[:, cols, :].rearrange("p c t -> p (c t)")
             )
-            nc.sync.dma_start(words_of(out_1)[:, cols], y_w[:, cols].bitcast(I32))
+            if c != 0:
+                stored = slice(0, h + width) if c == 1 else cols
+                nc.sync.dma_start(words_of(out_1)[:, stored], y_w[:, stored].bitcast(I32))
         for q in range(4):
             queue = nc.sync if q % 2 else nc.scalar
             queue.dma_start(out_2[0, 4 * q : 4 * q + 4, :].bitcast(I32), y_s[32 * q : 32 * q + 4, :].bitcast(I32))

@@ -83,8 +83,8 @@ def tile_picked_ckqkinddiflerp_none_po_kernel(
         load_scale_rows(nc.sync, w1_s, w1_scales)
         k1_l = load_list("k1_l", k1)
         nc.sync.dma_start(d_s[0:P:8, :].bitcast(I32), d_scales[0].bitcast(I32))
-        nc.sync.dma_start(d_w[:].bitcast(I32), words_of(d_words))
         offs_l = load_list("offs_l", offs)
+        nc.sync.dma_start(d_w[:].bitcast(I32), words_of(d_words))
         n3_l = load_list("n3_l", n3)
         n2_l = load_list("n2_l", n2)
         nc.sync.dma_start(tab_t[2][:, :N], tab_rows[:, 2, :])
@@ -96,6 +96,13 @@ def tile_picked_ckqkinddiflerp_none_po_kernel(
         abs_ga = sb("abs_ga", [P, PACK], F32)
         a_gain = sb("a_gain", [P, PACK], F32)
         b_gain = sb("b_gain", [P, PACK], F32)
+        step_a = sb("step_a", [P, PACK], F32)
+        sign_a = sb("sign_a", [P, PACK], F32)
+        nc.gpsimd.tensor_scalar(step_a[:], ga_t[:], 0.0, 2.0, ALU.is_ge, ALU.mult)
+        nc.gpsimd.tensor_scalar(sign_a[:], step_a[:], 1.0, -1.0, ALU.mult, ALU.add)
+        nc.gpsimd.tensor_tensor(b_gain[:], gb_t[:], sign_a[:], ALU.mult)
+        nc.gpsimd.tensor_tensor(abs_ga[:], ga_t[:], sign_a[:], ALU.mult)
+        nc.gpsimd.tensor_scalar(a_gain[:], abs_ga[:], SIXTEENTH, 0.0, ALU.mult, ALU.add)
 
         def deal(dst, src):
             nc.vector.tensor_copy(
@@ -125,12 +132,6 @@ def tile_picked_ckqkinddiflerp_none_po_kernel(
         w1_sd = sb("w1_sd", [P, N], U8)
         deal(w1_wd, w1_w)
         deal(w1_sd, w1_s)
-
-        half_sign = sb("half_sign", [P, PACK], F32, tag="w1_s")
-        nc.vector.tensor_scalar(half_sign[:], ga_t[:], 0.0, 0.5, ALU.is_ge, ALU.subtract)
-        nc.vector.scalar_tensor_tensor(b_gain[:], half_sign[:], 2.0, gb_t[:], ALU.mult, ALU.mult)
-        nc.vector.scalar_tensor_tensor(abs_ga[:], half_sign[:], 2.0, ga_t[:], ALU.mult, ALU.mult)
-        nc.vector.scalar_tensor_tensor(a_gain[:], half_sign[:], 2.0 * SIXTEENTH, ga_t[:], ALU.mult, ALU.mult)
 
         dk_s = pick("dk_s", d_s, k1_l, U8)
         dk_sd = sb("dk_sd", [P, N], U8)
@@ -218,7 +219,6 @@ def tile_picked_ckqkinddiflerp_none_po_kernel(
         diff = sb("diff", [P, PACK, N], F32)
         step = sb("step", [P, PACK, N], F32)
         y = sb("y", [P, PACK, N], F32)
-        y_h = sb("y_h", [P, N, PACK], BF16)
 
         def blend(t, c0, width):
             cols = slice(c0, c0 + width)
@@ -241,21 +241,32 @@ def tile_picked_ckqkinddiflerp_none_po_kernel(
             for h, width in ((0, HALF), (HALF, HALF)) if t == 0 else ((0, N),):
                 blend(t, h, width)
             nc.sync.dma_start(y_rows[:, t, :], y[:, t, :])
+
+        def weave(tile, cols):
+            return tile[:].rearrange("p (c i) t -> p c t i", i=4), y[:, :, cols].rearrange("p t (c i) -> p c t i", i=4)
+
+        def quantise(tile, cols):
+            nc.vector.quantize_mx(
+                out=y_w[:, cols].bitcast(FP8X4), scales=y_s[:, cols], in_=tile[:].rearrange("p c t -> p (c t)")
+            )
+
+        first, second = slice(0, HALF), slice(HALF, N)
         for c, (h, width) in enumerate(CHUNKS):
             blend(last, h, width)
             cols = slice(h, h + width)
-            if c != 1:
-                stored = slice(0, HALF) if c == 0 else slice(HALF, N)
-                nc.sync.dma_start(y_rows[:, last, stored], y[:, last, stored])
-            nc.vector.tensor_copy(
-                y_h[:, cols, :].rearrange("p (c i) t -> p c t i", i=4), y[:, :, cols].rearrange("p t (c i) -> p c t i", i=4)
-            )
-            nc.vector.quantize_mx(
-                out=y_w[:, cols].bitcast(FP8X4), scales=y_s[:, cols], in_=y_h[:, cols, :].rearrange("p c t -> p (c t)")
-            )
-            if c != 0:
-                stored = slice(0, h + width) if c == 1 else cols
-                nc.sync.dma_start(words_of(out_1)[:, stored], y_w[:, stored].bitcast(I32))
+            if c == 0:
+                nc.sync.dma_start(y_rows[:, last, first], y[:, last, first])
+                cols = slice(0, P)
+            if c == len(CHUNKS) - 1:
+                nc.sync.dma_start(y_rows[:, last, second], y[:, last, second])
+                y_late = sb("y_late", [P, P, PACK], BF16, tag="s_%d" % last)
+                nc.scalar.activation(*weave(y_late, slice(P, HALF)), ACT.Copy)
+            y_h = sb("y_h_%d" % c, [P, P, PACK], BF16)
+            nc.vector.tensor_copy(*weave(y_h, cols))
+            quantise(y_h, cols)
+        quantise(y_late, slice(P, HALF))
+        nc.scalar.dma_start(words_of(out_1)[:, second], y_w[:, second].bitcast(I32))
+        nc.sync.dma_start(words_of(out_1)[:, first], y_w[:, first].bitcast(I32))
         for q in range(4):
             queue = nc.sync if q % 2 else nc.scalar
             queue.dma_start(out_2[0, 4 * q : 4 * q + 4, :].bitcast(I32), y_s[32 * q : 32 * q + 4, :].bitcast(I32))

from contextlib import ExitStack

import concourse.mybir as mybir

F32 = mybir.dt.float32
BF16 = mybir.dt.bfloat16
I32 = mybir.dt.int32
U32 = mybir.dt.uint32
U16 = mybir.dt.uint16
U8 = mybir.dt.uint8
FP8X4 = mybir.dt.float8_e4m3fn_x4
ALU = mybir.AluOpType
ACT = mybir.ActivationFunctionType

P = 128
PACK = 4
N = 512
T = 1024
G = 2048
HALF = 256
SIXTEENTH = 0.0625
WIDE = 2 * N
GATE_FIRST = (0, 1, 2)
CHUNKS = ((0, 256), (256, 128), (384, 128))

FLOPS = 3 * 2 * 512 * 512 * 512


def tile_picked_ckqkinddiflerp_none_po_kernel(
    tc, x_words, x_scales, d_words, d_scales, w1_words, w1_scales, tab, ga, gb,
    offs, k1, two, n1, n2, n3, n4, n5, n6, out_0, out_1, out_2,
):
    nc = tc.nc
    with ExitStack() as ctx:
        keep = ctx.enter_context(tc.tile_pool(name="keep", bufs=1))
        psum = ctx.enter_context(tc.psum_pool(name="psum", bufs=1))

        def sb(name, shape, dtype, tag=None):
            return keep.tile(shape, dtype, name=name, tag=tag or name, align_bytes=64)

        def load_list(name, src):
            lst = keep.tile([P, N // 16], U16, name=name)
            nc.sync.dma_start(lst[:], src)
            return lst

        def words_of(src):
            return src[0].rearrange("p n r -> p (n r)").bitcast(I32)

        def entries(lst, start, count):
            return lst[:, start // 16 : (start + count) // 16]

        x_w = sb("x_w", [P, T], U32)
        d_w = sb("d_w", [P, G], U32)
        w1_w = sb("w1_w", [P, N], U32)
        x_s = sb("x_s", [P, T], U8)
        d_s = sb("d_s", [P, G], U8)
        w1_s = sb("w1_s", [P, N], U8)
        tab_t = [sb("tab_%d" % t, [P, WIDE], F32, tag="window_%d" % t) for t in range(PACK)]
        ga_t = sb("ga_t", [P, PACK], F32)
        gb_t = sb("gb_t", [P, PACK], F32)
        tab_rows = tab.rearrange("(p t) c -> p t c", t=PACK)

        warm = sb("warm", [P, 1], F32)
        nc.gpsimd.memset(x_s[:].bitcast(I32), 0)
        nc.gpsimd.memset(w1_s[:].bitcast(I32), 0)
        nc.vector.memset(warm[:], 0.0)
        nc.vector.memset(d_s[:].bitcast(I32), 0)

        def load_scale_rows(queue, plane, src):
            for q in range(4):
                queue.dma_start(plane[32 * q : 32 * q + 4, :].bitcast(I32), src[0, 4 * q : 4 * q + 4, :].bitcast(I32))

        load_scale_rows(nc.scalar, x_s, x_scales)
        nc.scalar.activation(warm[:], warm[:], ACT.Sigmoid)
        nc.gpsimd.dma_start(ga_t[:], ga.rearrange("(p t) o -> p (t o)", t=PACK))
        nc.gpsimd.dma_start(gb_t[:], gb.rearrange("(p t) o -> p (t o)", t=PACK))
        two_l = load_list("two_l", two)
        nc.sync.dma_start(x_w[:].bitcast(I32), words_of(x_words))
        n1_l = load_list("n1_l", n1)
        nc.sync.dma_start(tab_t[0][:, :N], tab_rows[:, 0, :])
        nc.sync.dma_start(w1_w[:].bitcast(I32), words_of(w1_words))
        nc.sync.dma_start(tab_t[1][:, :N], tab_rows[:, 1, :])
        load_scale_rows(nc.sync, w1_s, w1_scales)
        k1_l = load_list("k1_l", k1)
        nc.sync.dma_start(d_s[0:P:8, :].bitcast(I32), d_scales[0].bitcast(I32))
        offs_l = load_list("offs_l", offs)
        nc.sync.dma_start(d_w[:].bitcast(I32), words_of(d_words))
        n3_l = load_list("n3_l", n3)
        n2_l = load_list("n2_l", n2)
        nc.sync.dma_start(tab_t[2][:, :N], tab_rows[:, 2, :])
        nc.sync.dma_start(tab_t[3][:, :N], tab_rows[:, 3, :])
        n4_l = load_list("n4_l", n4)
        n6_l = load_list("n6_l", n6)
        n5_l = load_list("n5_l", n5)

        abs_ga = sb("abs_ga", [P, PACK], F32)
        a_gain = sb("a_gain", [P, PACK], F32)
        b_gain = sb("b_gain", [P, PACK], F32)
        step_a = sb("step_a", [P, PACK], F32)
        sign_a = sb("sign_a", [P, PACK], F32)
        nc.gpsimd.tensor_scalar(step_a[:], ga_t[:], 0.0, 2.0, ALU.is_ge, ALU.mult)
        nc.gpsimd.tensor_scalar(sign_a[:], step_a[:], 1.0, -1.0, ALU.mult, ALU.add)
        nc.gpsimd.tensor_tensor(b_gain[:], gb_t[:], sign_a[:], ALU.mult)
        nc.gpsimd.tensor_tensor(abs_ga[:], ga_t[:], sign_a[:], ALU.mult)
        nc.gpsimd.tensor_scalar(a_gain[:], abs_ga[:], SIXTEENTH, 0.0, ALU.mult, ALU.add)

        def deal(dst, src):
            nc.vector.tensor_copy(
                dst[:].rearrange("p (t m) -> p t m", t=PACK), src[:].rearrange("p (m t) -> p t m", t=PACK)
            )

        def pick(name, table, lst, dtype, tag=None):
            got = sb(name, [P, N], dtype, tag)
            nc.vector.tensor_copy(got[:], table[:].indirect(lst[:]))
            return got

        def product(bank, t, lhs_w, lhs_s, rhs_w, rhs_s):
            acc = psum.tile([P, N], F32, name="bank%d" % bank)
            cols = slice(P * t, P * (t + 1))
            nc.tensor.matmul_mx(
                out=acc[:], lhsT=lhs_w[:, cols].bitcast(FP8X4), lhsT_scale=lhs_s[:, cols],
                rhs=rhs_w[:].bitcast(FP8X4), rhs_scale=rhs_s[:], start=True, stop=True,
            )
            return acc

        def fetch(dst, window, lst, start, count, func):
            nc.scalar.activation(dst, window[:].indirect(entries(lst, start, count)), func)

        xt_s = pick("xt_s", x_s, two_l, U8)
        xt_w = pick("xt_w", x_w, two_l, U32)
        w1_wd = sb("w1_wd", [P, N], U32)
        w1_sd = sb("w1_sd", [P, N], U8)
        deal(w1_wd, w1_w)
        deal(w1_sd, w1_s)

        dk_s = pick("dk_s", d_s, k1_l, U8)
        dk_sd = sb("dk_sd", [P, N], U8)
        deal(dk_sd, dk_s)
        for r in range(1, 4):
            nc.sync.dma_start(dk_sd[r:P:32, :].bitcast(I32), dk_sd[8 * r : P : 32, :].bitcast(I32))

        tab_g = sb("tab_g", [P, PACK, N], F32)
        for t in range(2):
            fetch(tab_g[:, t, :], tab_t[t], n1_l, 0, N, ACT.Copy)

        b_acc = [product(t, t, w1_wd, w1_sd, xt_w, xt_s) for t in range(PACK)]

        xo_w = pick("xo_w", x_w, offs_l, U32, tag="held")
        xo_s = pick("xo_s", x_s, offs_l, U8)
        dk_w = pick("dk_w", d_w, k1_l, U32)
        dk_wd = sb("dk_wd", [P, N], U32)
        deal(dk_wd, dk_w)
        a_acc = [product(PACK + t, t, dk_wd, dk_sd, xo_w, xo_s) for t in range(PACK)]

        b_g = sb("b_g", [P, PACK, N], F32)
        for t in range(PACK):
            b_t = sb("b_%d" % t, [P, WIDE], F32, tag="window_%d" % (1 - t) if t < 2 else None)
            nc.scalar.activation(b_t[:, :N], b_acc[t][:], ACT.Copy, scale=b_gain[:, t : t + 1])
            fetch(b_g[:, t, :], b_t, n3_l, 0, N, ACT.Copy)
        for t in range(2, PACK):
            fetch(tab_g[:, t, :], tab_t[t], n1_l, 0, N, ACT.Copy)

        a_t = [sb("a_%d" % t, [P, N], F32) for t in range(PACK)]
        a_g = sb("a_g", [P, PACK, N], F32)
        a_sum = sb("a_sum", [P, PACK, N], F32)
        for t in range(PACK - 1):
            nc.vector.tensor_scalar(a_t[t][:], a_acc[t][:], a_gain[:, t : t + 1], None, ALU.mult)
        nc.scalar.activation(a_t[3][:], a_acc[3][:], ACT.Copy, scale=a_gain[:, 3:4])
        b_all = sb("b_all", [P, PACK, N], F32, tag="held")
        for t in range(PACK):
            nc.vector.scalar_tensor_tensor(
                b_all[:, t, :], b_acc[t][:], b_gain[:, t : t + 1], b_g[:, t, :], ALU.mult, ALU.subtract
            )
        for h, width in CHUNKS:
            for t in range(PACK):
                fetch(a_g[:, t, h : h + width], a_t[t], n2_l, h, width, ACT.Copy)
        nc.vector.scalar_tensor_tensor(a_sum[:, 0, :], tab_g[:, 0, :], abs_ga[:, 0:1], a_t[0][:], ALU.mult, ALU.add)
        z2_h = sb("z2_h", [P, N, PACK], BF16)
        nc.vector.tensor_copy(
            z2_h[:].rearrange("p (c i) t -> p c t i", i=4), b_all[:].rearrange("p t (c i) -> p c t i", i=4)
        )
        for t in range(1, PACK):
            nc.vector.scalar_tensor_tensor(
                a_sum[:, t, :], tab_g[:, t, :], abs_ga[:, t : t + 1], a_t[t][:], ALU.mult, ALU.add
            )
        z2_w = sb("z2_w", [P, N], U32)
        z2_s = sb("z2_s", [P, N], U8)
        nc.vector.quantize_mx(out=z2_w[:].bitcast(FP8X4), scales=z2_s[:], in_=z2_h[:].rearrange("p c t -> p (c t)"))

        z_h = sb("z_h", [P, PACK, P, PACK], BF16)
        for h, width in CHUNKS:
            m = slice(h // PACK, (h + width) // PACK)
            nc.vector.tensor_tensor(
                z_h[:, :, m, :].rearrange("p u m t -> p m t u"),
                a_sum[:, :, h : h + width].rearrange("p t (m u) -> p m t u", u=PACK),
                a_g[:, :, h : h + width].rearrange("p t (m u) -> p m t u", u=PACK),
                ALU.max,
            )
        z_w = sb("z_w", [P, N], U32)
        z_s = sb("z_s", [P, N], U8)
        for u in range(PACK):
            cols = slice(P * u, P * (u + 1))
            nc.vector.quantize_mx(
                out=z_w[:, cols].bitcast(FP8X4), scales=z_s[:, cols], in_=z_h[:, u].rearrange("p m t -> p (m t)")
            )

        s_t = [sb("s_%d" % t, [P, WIDE if t in GATE_FIRST else N], F32) for t in range(PACK)]
        s_acc = [product(t, t, z_w, z_s, z2_w, z2_s) for t in range(PACK)]
        nc.scalar.activation(s_t[0][:, :N], s_acc[0][:], ACT.Copy, scale=SIXTEENTH)
        for t in range(1, PACK):
            nc.vector.tensor_scalar(s_t[t][:, :N], s_acc[t][:], SIXTEENTH, None, ALU.mult)

        y_rows = out_0.rearrange("(p t) c -> p t c", t=PACK)
        y_w = sb("y_w", [P, N], U32)
        y_s = sb("y_s", [P, N], U8)
        near = sb("near", [P, PACK, N], F32)
        far = sb("far", [P, PACK, N], F32)
        gate = sb("gate", [P, PACK, N], F32)
        diff = sb("diff", [P, PACK, N], F32)
        step = sb("step", [P, PACK, N], F32)
        y = sb("y", [P, PACK, N], F32)

        def blend(t, c0, width):
            cols = slice(c0, c0 + width)
            fetch(near[:, t, cols], s_t[t], n4_l, c0, width, ACT.Copy)
            fetch(far[:, t, cols], s_t[t], n6_l, c0, width, ACT.Copy)
            nc.vector.tensor_tensor(diff[:, t, cols], far[:, t, cols], near[:, t, cols], ALU.subtract)
            if t in GATE_FIRST:
                nc.vector.tensor_tensor(
                    step[:, t, cols], gate_t[t][:].indirect(entries(n5_l, c0, width)), diff[:, t, cols], ALU.mult
                )
            else:
                fetch(gate[:, t, cols], s_t[t], n5_l, c0, width, ACT.Sigmoid)
                nc.vector.tensor_tensor(step[:, t, cols], diff[:, t, cols], gate[:, t, cols], ALU.mult)
            nc.vector.tensor_tensor(y[:, t, cols], step[:, t, cols], near[:, t, cols], ALU.add)

        last = PACK - 1
        gate_t = [sb("gate_%d" % t, [P, WIDE], F32) for t in GATE_FIRST]
        for t in range(last):
            nc.scalar.activation(gate_t[t][:, :N], s_acc[t][:], ACT.Sigmoid, scale=SIXTEENTH)
            for h, width in ((0, HALF), (HALF, HALF)) if t == 0 else ((0, N),):
                blend(t, h, width)
            nc.sync.dma_start(y_rows[:, t, :], y[:, t, :])

        def weave(tile, cols):
            return tile[:].rearrange("p (c i) t -> p c t i", i=4), y[:, :, cols].rearrange("p t (c i) -> p c t i", i=4)

        def quantise(tile, cols):
            nc.vector.quantize_mx(
                out=y_w[:, cols].bitcast(FP8X4), scales=y_s[:, cols], in_=tile[:].rearrange("p c t -> p (c t)")
            )

        first, second = slice(0, HALF), slice(HALF, N)
        for c, (h, width) in enumerate(CHUNKS):
            blend(last, h, width)
            cols = slice(h, h + width)
            if c == 0:
                nc.sync.dma_start(y_rows[:, last, first], y[:, last, first])
                cols = slice(0, P)
            if c == len(CHUNKS) - 1:
                nc.sync.dma_start(y_rows[:, last, second], y[:, last, second])
                y_late = sb("y_late", [P, P, PACK], BF16, tag="s_%d" % last)
                nc.scalar.activation(*weave(y_late, slice(P, HALF)), ACT.Copy)
            y_h = sb("y_h_%d" % c, [P, P, PACK], BF16)
            nc.vector.tensor_copy(*weave(y_h, cols))
            quantise(y_h, cols)
        quantise(y_late, slice(P, HALF))
        nc.scalar.dma_start(words_of(out_1)[:, second], y_w[:, second].bitcast(I32))
        nc.sync.dma_start(words_of(out_1)[:, first], y_w[:, first].bitcast(I32))
        for q in range(4):
            queue = nc.sync if q % 2 else nc.scalar
            queue.dma_start(out_2[0, 4 * q : 4 * q + 4, :].bitcast(I32), y_s[32 * q : 32 * q + 4, :].bitcast(I32))
